import numpy as np
import ml_dtypes


def mxq(x, axis, fmt="e4m3"):
    dtype, down = {"e4m3": (ml_dtypes.float8_e4m3fn, 7), "e5m2": (ml_dtypes.float8_e5m2, 14)}[fmt]
    v = np.moveaxis(np.asarray(x, np.float32).astype(ml_dtypes.bfloat16).astype(np.float64), axis, -1)
    blocks = v.reshape(v.shape[:-1] + (-1, 32))
    amax = np.abs(blocks).max(-1, keepdims=True)
    byte = np.maximum(np.where(amax > 0, np.frexp(amax)[1] - 1 + 127, 0) - down, 1)
    scale = np.exp2(byte - 127.0)
    codes = (blocks / scale).astype(np.float32).astype(dtype).astype(np.float64)
    return np.moveaxis((codes * scale).reshape(v.shape), -1, axis)


WIDE = False


def mx_kscale(k):
    if not WIDE:
        return np.ones(k)
    levels = np.array([10, -10, 5, -5, 0])
    if k % 512:
        return np.exp2(np.random.permutation(np.resize(levels, k // 32))).repeat(32)
    a = np.empty((k // 512, 16))
    for p in range(k // 512):
        a[p, :8] = np.random.permutation(np.resize(levels, 8))
        for g in range(8):
            far = levels[np.abs(levels - a[p, g]) >= 10]
            a[p, g + 8] = far[np.random.randint(len(far))]
    return np.exp2(a.ravel()).repeat(32)


BF16 = ml_dtypes.bfloat16


def bf(x):
    return np.asarray(x, np.float32).astype(BF16)


def f64(x):
    return np.asarray(x).astype(np.float64)


E2M1 = np.array([0.0, 0.5, 1.0, 1.5, 2.0, 3.0, 4.0, 6.0, -0.0, -0.5, -1.0, -1.5, -2.0, -3.0, -4.0, -6.0])


def pack_weight(w, fmt):
    k, n = w.shape
    w = f64(bf(w)).reshape(k // 32, 32, n)
    amax = np.abs(w).max(1)
    if fmt == "e4m3":
        byte = np.frexp(amax)[1] - 1 + 127 - 7
    else:
        mant, ex = np.frexp(amax / 6.0)
        byte = np.where(mant > 0.5, ex, ex - 1) + 127
    byte = np.clip(np.where(amax > 0, byte, 1), 1, 254)
    scaled = (w * np.exp2(127.0 - byte)[:, None, :]).reshape(k, n).astype(np.float32)
    by_word = np.ascontiguousarray(scaled.reshape(k // 512, 128, 4, n).transpose(0, 1, 3, 2))
    if fmt == "e4m3":
        words = by_word.astype(ml_dtypes.float8_e4m3fn).view(np.uint8)
    else:
        c = by_word.astype(ml_dtypes.float4_e2m1fn).view(np.uint8) & 0xF
        words = c[..., 0::2] | (c[..., 1::2] << 4)
    return np.ascontiguousarray(words), np.ascontiguousarray(byte.astype(np.uint8).reshape(k // 512, 16, n))


def unpack_weight(words, scales, fmt):
    g, p, n, _ = words.shape
    if fmt == "e4m3":
        vals = np.ascontiguousarray(words).view(ml_dtypes.float8_e4m3fn).astype(np.float64)
    else:
        nib = np.empty((g, p, n, 4), np.uint8)
        nib[..., 0::2] = words & 0xF
        nib[..., 1::2] = words >> 4
        vals = E2M1[nib]
    vals = vals * np.repeat(np.exp2(scales.astype(np.float64) - 127.0), 8, axis=1)[..., None]
    return vals.transpose(0, 1, 3, 2).reshape(g * 512, n)
def pack4(w):
    words, scales = pack_weight(w, "e2m1")
    return words.reshape(words.shape[0], 128, -1), scales


def unpack4(words, scales):
    return unpack_weight(words.reshape(words.shape[0], 128, -1, 2), scales, "e2m1")


T, A, E, P, R = 512, 512, 2048, 1024, 1024


def draw0():
    s = mx_kscale(A)
    u = mx_kscale(P)
    t = mx_kscale(E)
    resp = np.random.standard_normal((P, E)) / np.sqrt(P) / u[:, None] / t
    resp_words, resp_scales = pack4(resp)
    return {"sig": bf(np.random.standard_normal((T, A)) * s),
            "inc": bf(np.random.standard_normal((A, E)) / np.sqrt(A) / s[:, None]),
            "bias": bf(0.3 * np.random.standard_normal(E)),
            "gain": bf((1 + 0.2 * np.random.standard_normal(E)) * t),
            "coef": bf(np.random.standard_normal((R, P)) * E ** -0.25 * u),
            "resp_words": resp_words,
            "resp_scales": resp_scales}


def core(sig, inc, bias, gain, coef, resp_words, resp_scales):
    field = mxq(f64(sig), 1, "e4m3") @ mxq(f64(inc), 0, "e4m3")
    refl = f64(gain) * np.tanh(field + f64(bias))
    outgoing = mxq(f64(coef), 1, "e4m3") @ unpack4(resp_words, resp_scales)
    return mxq(refl, 1, "e4m3") @ mxq(outgoing, 1, "e4m3").T


def e4m3fn_bytes(y):
    return np.clip(np.asarray(y, np.float64), -448.0, 448.0).astype(np.float32).astype(ml_dtypes.float8_e4m3fn).view(np.uint8)


def e4m3fn_values(b):
    return np.asarray(b, np.uint8).view(ml_dtypes.float8_e4m3fn).astype(np.float64)


def setup_inputs():
    d = draw0()
    x0 = np.asarray(d['inc']).astype(np.float64)
    s = (np.max(np.abs(x0), axis=(1,), keepdims=True) / 448.0).astype(np.float32)
    out = {}
    for k, v in d.items():
        if k == 'inc':
            out['inc_bytes'] = e4m3fn_bytes(x0 / s.astype(np.float64))
            out['inc_scale'] = s
        else:
            out[k] = v
    return out


def reference(sig, inc_bytes, inc_scale, bias, gain, coef, resp_words, resp_scales):
    return core(sig, e4m3fn_values(inc_bytes) * inc_scale.astype(np.float64), bias, gain, coef, resp_words, resp_scales)

@@ -1,0 +1,399 @@
+from contextlib import ExitStack
+
+import concourse.mybir as mybir
+from concourse.masks import make_identity
+
+T, A, E, PATHS, R = 512, 512, 2048, 1024, 1024
+FLOPS = 2 * (T * A * E + R * PATHS * E + T * E * R)
+
+F32 = mybir.dt.float32
+BF16 = mybir.dt.bfloat16
+I32 = mybir.dt.int32
+U32 = mybir.dt.uint32
+U8 = mybir.dt.uint8
+FP8 = mybir.dt.float8_e4m3fn
+FP8X4 = mybir.dt.float8_e4m3fn_x4
+FP4X4 = mybir.dt.float4_e2m1fn_x4
+MULT = mybir.AluOpType.mult
+TANH = mybir.ActivationFunctionType.Tanh
+
+P = 128
+GROUPS = E // 512
+N_COEF = R // 128
+HALF_R = 512
+
+
+def tile_active_surface_link_s11_kernel(
+    tc, sig, inc_bytes, inc_scale, bias, gain, coef, resp_words, resp_scales, out
+):
+    nc = tc.nc
+    with ExitStack() as ctx:
+        keep = ctx.enter_context(tc.tile_pool(name="keep", bufs=1))
+        work = ctx.enter_context(tc.tile_pool(name="work", bufs=2))
+        rot = ctx.enter_context(tc.psum_pool(name="rot", bufs=4))
+        acc = ctx.enter_context(tc.psum_pool(name="acc", bufs=4))
+        ctx.enter_context(tc.manual_schedule())
+
+        def kept(name, shape, dtype):
+            return keep.tile(shape, dtype, name=name, tag=name, align_bytes=64)
+
+        coef_raw = [kept("coef_raw%d" % n, [P, PATHS], BF16) for n in range(N_COEF)]
+        coef_codes = [kept("coef_codes%d" % n, [P, 2, 128], U32) for n in range(N_COEF)]
+        coef_scales = [kept("coef_scales%d" % n, [P, 2, 128], U8) for n in range(N_COEF)]
+        resp_raw = [kept("resp_raw%d" % h, [P, 2, E], U8) for h in range(2)]
+        resp_perm = [kept("resp_perm%d" % h, [P, 2, E], U8) for h in range(2)]
+        rs_raw = kept("rs_raw", [P, 2, E], U8)
+        rs_perm = kept("rs_perm", [P, 2, E], U8)
+        inc_b = [kept("inc_b%d" % h, [P, 4, E // 2], U8) for h in range(2)]
+        inc_sc = kept("inc_sc", [P, 4], F32)
+        inc_codes = [kept("inc_codes%d" % g, [P, 512], U32) for g in range(GROUPS)]
+        inc_scales = [kept("inc_scales%d" % g, [P, 512], U8) for g in range(GROUPS)]
+        sig_raw = kept("sig_raw", [P, 4, A], BF16)
+        sig_grp = kept("sig_grp", [P, T, 4], BF16)
+        sig_codes = kept("sig_codes", [P, T], U32)
+        sig_scales = kept("sig_scales", [P, T], U8)
+        refl_codes = [kept("refl_codes%d" % g, [P, T], U32) for g in range(GROUPS)]
+        refl_scales = [kept("refl_scales%d" % g, [P, T], U8) for g in range(GROUPS)]
+        outg_codes = [[kept("outg_codes%d_%d" % (h, g), [P, HALF_R], U32) for g in range(GROUPS)] for h in range(2)]
+        outg_scales = [[kept("outg_scales%d_%d" % (h, g), [P, HALF_R], U8) for g in range(GROUPS)] for h in range(2)]
+        ident = kept("ident", [P, P], F32)
+        vec_b = kept("vec_b", [P, P], BF16)
+        vec_f = kept("vec_f", [P, P], F32)
+        vec_t = kept("vec_t", [P, 32], F32)
+        dummy = kept("dummy", [P, 1], F32)
+
+        nc.vector.memset(rs_raw[:].rearrange("p g e -> p (g e)").bitcast(I32), 0)
+        nc.vector.memset(dummy[:], 0.0)
+        make_identity(nc, ident[:])
+        nc.gpsimd.memset(vec_b[:], 0.0)
+        nc.scalar.activation(dummy[:], dummy[:], TANH)
+
+        def load_coef(n):
+            nc.sync.dma_start(out=coef_raw[n][:], in_=coef[128 * n : 128 * (n + 1), :])
+
+        def load_resp(h):
+            nc.sync.dma_start(
+                out=resp_raw[h][:].bitcast(I32),
+                in_=resp_words[:, :, E * h : E * (h + 1)].rearrange("g p b -> p g b").bitcast(I32),
+            )
+
+        def load_inc(h):
+            cols = slice(E // 2 * h, E // 2 * (h + 1))
+            nc.sync.dma_start(out=inc_b[h][:], in_=inc_bytes[:, cols].rearrange("(p j) e -> p j e", j=4))
+
+        load_coef(0)
+        load_coef(1)
+        for q in range(4):
+            nc.sync.dma_start(
+                out=rs_raw[32 * q : 32 * q + 4, :, :].bitcast(I32),
+                in_=resp_scales[:, 4 * q : 4 * q + 4, :].rearrange("g q e -> q g e").bitcast(I32),
+            )
+        load_resp(0)
+        load_resp(1)
+        load_coef(2)
+        load_coef(3)
+        nc.sync.dma_start(out=inc_sc[:], in_=inc_scale.rearrange("(p j) o -> p (j o)", j=4))
+        load_inc(0)
+        nc.sync.dma_start(out=sig_raw[:], in_=sig.rearrange("(n p) a -> p n a", p=P))
+        load_inc(1)
+        for n in range(4, N_COEF):
+            load_coef(n)
+        for v, vec in enumerate((bias, gain)):
+            for g in range(GROUPS):
+                row = 16 * v + 4 * g
+                nc.scalar.dma_start(
+                    out=vec_b[row : row + 4, :].rearrange("r (q i) -> r q i", i=8),
+                    in_=vec[512 * g : 512 * (g + 1)].rearrange("(q t i) -> t q i", t=4, i=8),
+                )
+
+        coef_bank, coef_grp = {}, {}
+
+        def t_coef(n, pool):
+            bank = pool.tile([P, 512], F32, name="bank", tag="bank")
+            words = coef_raw[n][:].bitcast(F32)
+            for g in range(2):
+                for u in range(2):
+                    j = 2 * g + u
+                    nc.tensor.transpose(
+                        bank[:, 128 * j : 128 * (j + 1)], words[:, 256 * g + u : 256 * (g + 1) : 2], ident[:]
+                    )
+            coef_bank[n] = bank
+
+        def copy(engine, dst, src):
+            if engine == "v":
+                nc.vector.tensor_copy(out=dst, in_=src)
+            else:
+                nc.scalar.copy(out=dst, in_=src)
+
+        def c_coef(n, engine):
+            grp = work.tile([P, 2, 128, 4], BF16, name="coef_grp", tag="coef_grp", bufs=4, align_bytes=64)
+            coef_grp[n] = grp
+            copy(
+                engine,
+                grp[:].rearrange("p g r t -> p (g r t)").bitcast(F32).rearrange("p (g r u) -> p g r u", g=2, u=2),
+                coef_bank[n][:].rearrange("p (g u r) -> p g r u", g=2, u=2),
+            )
+
+        def q_coef(n):
+            nc.vector.quantize_mx(
+                out=coef_codes[n][:].rearrange("p g r -> p (g r)").bitcast(FP8X4),
+                scales=coef_scales[n][:].rearrange("p g r -> p (g r)"),
+                in_=coef_grp[n][:].rearrange("p g r t -> p (g r t)"),
+            )
+
+        sig_bank = {}
+
+        def t_sig(pair, pool):
+            bank = pool.tile([P, 512], F32, name="bank", tag="bank")
+            for i in range(2):
+                words = sig_raw[:, 2 * pair + i, :].bitcast(F32)
+                for u in range(2):
+                    j = 2 * i + u
+                    nc.tensor.transpose(bank[:, 128 * j : 128 * (j + 1)], words[:, u:256:2], ident[:])
+            sig_bank[pair] = bank
+
+        def c_sig(pair, engine):
+            dst = sig_grp[:, 256 * pair : 256 * (pair + 1), :].rearrange("p r t -> p (r t)").bitcast(F32)
+            copy(
+                engine,
+                dst.rearrange("p (i r u) -> p i r u", i=2, u=2),
+                sig_bank[pair][:].rearrange("p (i u r) -> p i r u", i=2, u=2),
+            )
+
+        def q_sig():
+            nc.vector.quantize_mx(
+                out=sig_codes[:].bitcast(FP8X4), scales=sig_scales[:], in_=sig_grp[:].rearrange("p r t -> p (r t)")
+            )
+
+        def perm_scales(g):
+            nc.vector.tensor_copy(
+                out=rs_perm[:, g, :].bitcast(I32).rearrange("p (t b w) -> p t b w", t=4, w=2),
+                in_=rs_raw[:, g, :].bitcast(I32).rearrange("p (b t w) -> p t b w", t=4, w=2),
+            )
+
+        def perm_resp(h, g):
+            nc.vector.tensor_copy(
+                out=resp_perm[h][:, g, :].bitcast(I32).rearrange("p (t b w) -> p t b w", t=4, w=4),
+                in_=resp_raw[h][:, g, :].bitcast(I32).rearrange("p (b t w) -> p t b w", t=4, w=4),
+            )
+
+        inc_wid, inc_grp = {}, {}
+
+        def widen(grp):
+            wid = work.tile([P, 4, 512], BF16, name="inc_wid", tag="inc_wid", align_bytes=64)
+            inc_wid[grp] = wid
+            lo = 512 * (grp % 2)
+            for j in range(4):
+                nc.vector.tensor_scalar(
+                    out=wid[:, j, :].rearrange("p (t q i) -> p q t i", t=4, i=8),
+                    in0=inc_b[grp // 2][:, j, lo : lo + 512].bitcast(FP8).rearrange("p (q t i) -> p q t i", t=4, i=8),
+                    scalar1=inc_sc[:, j : j + 1],
+                    scalar2=None,
+                    op0=MULT,
+                )
+
+        def interleave(grp):
+            g4 = work.tile([P, 512, 4], BF16, name="inc_grp", tag="inc_grp", align_bytes=64)
+            inc_grp[grp] = g4
+            nc.vector.tensor_copy(
+                out=g4[:].rearrange("p (c i) j -> p c j i", i=4),
+                in_=inc_wid[grp][:].rearrange("p j (c i) -> p c j i", i=4),
+            )
+
+        def q_inc(grp):
+            nc.vector.quantize_mx(
+                out=inc_codes[grp][:].bitcast(FP8X4),
+                scales=inc_scales[grp][:],
+                in_=inc_grp[grp][:].rearrange("p c j -> p (c j)"),
+            )
+
+        outg = {}
+
+        def outgoing(n, grp, engine):
+            h = n // 4
+            if (h, grp) not in outg:
+                outg[(h, grp)] = work.tile(
+                    [P, HALF_R, 4], BF16, name="outg", tag="outg", bufs=6, align_bytes=64
+                )
+            bank = rot.tile([P, 512], F32, name="bank", tag="bank")
+            half, local = grp // 2, grp % 2
+            for t in range(4):
+                lo = 512 * t + 256 * local
+                so = 512 * t + 128 * grp
+                for g in range(2):
+                    nc.tensor.matmul_mx(
+                        out=bank[:, 128 * t : 128 * (t + 1)],
+                        lhsT=resp_perm[half][:, g, lo : lo + 256].bitcast(FP4X4),
+                        lhsT_scale=rs_perm[:, g, so : so + 128],
+                        rhs=coef_codes[n][:, g, :].bitcast(FP8X4),
+                        rhs_scale=coef_scales[n][:, g, :],
+                        start=(g == 0),
+                        stop=(g == 1),
+                    )
+            r0 = 128 * (n % 4)
+            copy(engine, outg[(h, grp)][:, r0 : r0 + 128, :], bank[:].rearrange("p (t r) -> p r t", t=4))
+
+        def q_outg(h, grp):
+            nc.vector.quantize_mx(
+                out=outg_codes[h][grp][:].bitcast(FP8X4),
+                scales=outg_scales[h][grp][:],
+                in_=outg[(h, grp)][:].rearrange("p r t -> p (r t)"),
+            )
+
+        refl_tanh, refl_grp = {}, {}
+
+        def field(grp):
+            th = work.tile([P, 4, T], F32, name="th", tag="th", bufs=3, align_bytes=64)
+            refl_tanh[grp] = th
+            for t in range(4):
+                bank = rot.tile([P, 512], F32, name="bank", tag="bank")
+                nc.tensor.matmul_mx(
+                    out=bank[:],
+                    lhsT=inc_codes[grp][:, 128 * t : 128 * (t + 1)].bitcast(FP8X4),
+                    lhsT_scale=inc_scales[grp][:, 128 * t : 128 * (t + 1)],
+                    rhs=sig_codes[:].bitcast(FP8X4),
+                    rhs_scale=sig_scales[:],
+                    start=True,
+                    stop=True,
+                )
+                col = 4 * grp + t
+                nc.scalar.activation(th[:, t, :], bank[:], TANH, bias=vec_t[:, col : col + 1])
+
+        def apply_gain(grp):
+            rf = work.tile([P, T, 4], BF16, name="refl", tag="refl", bufs=2, align_bytes=64)
+            refl_grp[grp] = rf
+            col = 16 + 4 * grp
+            nc.vector.tensor_tensor(
+                out=rf[:],
+                in0=refl_tanh[grp][:].rearrange("p t n -> p n t"),
+                in1=vec_t[:, col : col + 4].unsqueeze(1).to_broadcast([P, T, 4]),
+                op=MULT,
+            )
+
+        def q_refl(grp):
+            nc.vector.quantize_mx(
+                out=refl_codes[grp][:].bitcast(FP8X4),
+                scales=refl_scales[grp][:],
+                in_=refl_grp[grp][:].rearrange("p n t -> p (n t)"),
+            )
+
+        def final_pass(h, m, grp, bank):
+            cols = slice(128 * m, 128 * (m + 1))
+            nc.tensor.matmul_mx(
+                out=bank[:],
+                lhsT=refl_codes[grp][:, cols].bitcast(FP8X4),
+                lhsT_scale=refl_scales[grp][:, cols],
+                rhs=outg_codes[h][grp][:].bitcast(FP8X4),
+                rhs_scale=outg_scales[h][grp][:],
+                start=(grp == 0),
+                stop=(grp == GROUPS - 1),
+            )
+
+        def store(h, m, bank, engine):
+            res = work.tile([P, HALF_R], F32, name="res", tag="res", bufs=4, align_bytes=64)
+            copy(engine, res[:], bank[:])
+            nc.sync.dma_start(out=out[128 * m : 128 * (m + 1), HALF_R * h : HALF_R * (h + 1)], in_=res[:])
+
+        t_coef(0, acc)
+        t_coef(1, acc)
+        c_coef(0, "v")
+        c_coef(1, "s")
+        q_coef(0)
+        q_coef(1)
+        perm_scales(0)
+        perm_scales(1)
+        perm_resp(0, 0)
+        perm_resp(0, 1)
+        for n in (0, 1):
+            for grp in (0, 1):
+                outgoing(n, grp, "s")
+        perm_resp(1, 0)
+        perm_resp(1, 1)
+        nc.vector.tensor_copy(out=vec_f[:], in_=vec_b[:])
+        for n in (0, 1):
+            for grp in (2, 3):
+                outgoing(n, grp, "s")
+        t_coef(2, acc)
+        t_coef(3, acc)
+        t_sig(0, acc)
+        t_sig(1, acc)
+        vbank = rot.tile([P, 512], F32, name="bank", tag="bank")
+        nc.tensor.transpose(vbank[:, 0:128], vec_f[:], ident[:])
+        widen(0)
+        c_coef(2, "s")
+        c_coef(3, "s")
+        interleave(0)
+        q_coef(2)
+        q_coef(3)
+        c_sig(0, "v")
+        c_sig(1, "v")
+        nc.vector.tensor_copy(out=vec_t[:], in_=vbank[:, 0:32])
+        q_inc(0)
+        q_sig()
+        widen(1)
+        interleave(1)
+        for grp in range(4):
+            outgoing(2, grp, "s")
+        field(0)
+        widen(2)
+        q_inc(1)
+        interleave(2)
+        outgoing(3, 0, "s")
+        outgoing(3, 1, "s")
+        field(1)
+        apply_gain(0)
+        q_inc(2)
+        outgoing(3, 2, "s")
+        outgoing(3, 3, "s")
+        q_refl(0)
+        q_outg(0, 0)
+        apply_gain(1)
+        q_outg(0, 1)
+        for n in range(4, 8):
+            t_coef(n, acc)
+        c_coef(4, "s")
+        c_coef(5, "v")
+        c_coef(6, "s")
+        c_coef(7, "v")
+        q_coef(4)
+        q_coef(5)
+        q_coef(6)
+        q_coef(7)
+        q_refl(1)
+        q_outg(0, 2)
+        q_outg(0, 3)
+        widen(3)
+        for n in range(4, 8):
+            outgoing(n, 0, "s")
+        interleave(3)
+        field(2)
+        q_outg(1, 0)
+        q_inc(3)
+        for n in range(4, 8):
+            outgoing(n, 1, "s")
+        fin = [acc.tile([P, 512], F32, name="bank", tag="bank") for m in range(4)]
+        for grp in (0, 1):
+            for m in range(4):
+                final_pass(0, m, grp, fin[m])
+        apply_gain(2)
+        q_outg(1, 1)
+        field(3)
+        for n in range(4, 8):
+            outgoing(n, 2, "s")
+        q_refl(2)
+        apply_gain(3)
+        q_outg(1, 2)
+        q_refl(3)
+        for n in range(4, 8):
+            outgoing(n, 3, "v" if n % 2 else "s")
+        for grp in (2, 3):
+            for m in range(4):
+                final_pass(0, m, grp, fin[m])
+        q_outg(1, 3)
+        for m in range(4):
+            store(0, m, fin[m], "v" if m % 2 else "s")
+        for m in range(4):
+            bank = rot.tile([P, 512], F32, name="bank", tag="bank")
+            for grp in range(GROUPS):
+                final_pass(1, m, grp, bank)
+            store(1, m, bank, "v" if m % 2 else "s")

@@ -40,11 +40,11 @@ def tile_active_surface_link_s11_kernel(
         coef_raw = [kept("coef_raw%d" % n, [P, PATHS], BF16) for n in range(N_COEF)]
         coef_codes = [kept("coef_codes%d" % n, [P, 2, 128], U32) for n in range(N_COEF)]
         coef_scales = [kept("coef_scales%d" % n, [P, 2, 128], U8) for n in range(N_COEF)]
-        resp_raw = [kept("resp_raw%d" % h, [P, 2, E], U8) for h in range(2)]
-        resp_perm = [kept("resp_perm%d" % h, [P, 2, E], U8) for h in range(2)]
+        resp_raw = [kept("resp_raw%d" % g, [P, 2, 1024], U8) for g in range(GROUPS)]
+        resp_perm = [kept("resp_perm%d" % g, [P, 2, 1024], U8) for g in range(GROUPS)]
         rs_raw = kept("rs_raw", [P, 2, E], U8)
         rs_perm = kept("rs_perm", [P, 2, E], U8)
-        inc_b = [kept("inc_b%d" % h, [P, 4, E // 2], U8) for h in range(2)]
+        inc_b = [kept("inc_b%d" % g, [P, 4, 512], U8) for g in range(GROUPS)]
         inc_sc = kept("inc_sc", [P, 4], F32)
         inc_codes = [kept("inc_codes%d" % g, [P, 512], U32) for g in range(GROUPS)]
         inc_scales = [kept("inc_scales%d" % g, [P, 512], U8) for g in range(GROUPS)]
@@ -57,32 +57,37 @@ def tile_active_surface_link_s11_kernel(
         outg_codes = [[kept("outg_codes%d_%d" % (h, g), [P, HALF_R], U32) for g in range(GROUPS)] for h in range(2)]
         outg_scales = [[kept("outg_scales%d_%d" % (h, g), [P, HALF_R], U8) for g in range(GROUPS)] for h in range(2)]
         ident = kept("ident", [P, P], F32)
-        vec_b = kept("vec_b", [P, P], BF16)
-        vec_f = kept("vec_f", [P, P], F32)
-        vec_t = kept("vec_t", [P, 32], F32)
+        ident_b = kept("ident_b", [P, P], BF16)
+        vec_b = kept("vec_b", [P, 512], BF16)
+        vec_t = kept("vec_t", [P, GROUPS, 8], F32)
         dummy = kept("dummy", [P, 1], F32)
 
         nc.vector.memset(rs_raw[:].rearrange("p g e -> p (g e)").bitcast(I32), 0)
         nc.vector.memset(dummy[:], 0.0)
         make_identity(nc, ident[:])
         nc.gpsimd.memset(vec_b[:], 0.0)
+        make_identity(nc, ident_b[:])
         nc.scalar.activation(dummy[:], dummy[:], TANH)
 
         def load_coef(n):
             nc.sync.dma_start(out=coef_raw[n][:], in_=coef[128 * n : 128 * (n + 1), :])
 
-        def load_resp(h):
+        def load_resp(grp):
             nc.sync.dma_start(
-                out=resp_raw[h][:].bitcast(I32),
-                in_=resp_words[:, :, E * h : E * (h + 1)].rearrange("g p b -> p g b").bitcast(I32),
+                out=resp_raw[grp][:].bitcast(I32),
+                in_=resp_words[:, :, 1024 * grp : 1024 * (grp + 1)].rearrange("g p b -> p g b").bitcast(I32),
             )
 
-        def load_inc(h):
-            cols = slice(E // 2 * h, E // 2 * (h + 1))
-            nc.sync.dma_start(out=inc_b[h][:], in_=inc_bytes[:, cols].rearrange("(p j) e -> p j e", j=4))
+        def load_inc(grp):
+            cols = slice(512 * grp, 512 * (grp + 1))
+            nc.sync.dma_start(out=inc_b[grp][:], in_=inc_bytes[:, cols].rearrange("(p j) e -> p j e", j=4))
 
+        for v, vec in enumerate((bias, gain)):
+            nc.scalar.dma_start(
+                out=vec_b[4 * v : 4 * v + 4, :].rearrange("t (b i) -> t b i", i=8),
+                in_=vec.rearrange("(b t i) -> t b i", t=4, i=8),
+            )
         load_coef(0)
-        load_coef(1)
         for q in range(4):
             nc.sync.dma_start(
                 out=rs_raw[32 * q : 32 * q + 4, :, :].bitcast(I32),
@@ -90,21 +95,21 @@ def tile_active_surface_link_s11_kernel(
             )
         load_resp(0)
         load_resp(1)
-        load_coef(2)
-        load_coef(3)
         nc.sync.dma_start(out=inc_sc[:], in_=inc_scale.rearrange("(p j) o -> p (j o)", j=4))
         load_inc(0)
-        nc.sync.dma_start(out=sig_raw[:], in_=sig.rearrange("(n p) a -> p n a", p=P))
+        load_coef(1)
+        load_resp(2)
+        load_resp(3)
         load_inc(1)
-        for n in range(4, N_COEF):
-            load_coef(n)
-        for v, vec in enumerate((bias, gain)):
-            for g in range(GROUPS):
-                row = 16 * v + 4 * g
-                nc.scalar.dma_start(
-                    out=vec_b[row : row + 4, :].rearrange("r (q i) -> r q i", i=8),
-                    in_=vec[512 * g : 512 * (g + 1)].rearrange("(q t i) -> t q i", t=4, i=8),
-                )
+        load_coef(2)
+        load_coef(3)
+        nc.sync.dma_start(out=sig_raw[:], in_=sig.rearrange("(n p) a -> p n a", p=P))
+        load_inc(2)
+        load_inc(3)
+        load_coef(4)
+        load_coef(5)
+        load_coef(6)
+        load_coef(7)
 
         coef_bank, coef_grp = {}, {}
 
@@ -171,22 +176,29 @@ def tile_active_surface_link_s11_kernel(
                 in_=rs_raw[:, g, :].bitcast(I32).rearrange("p (b t w) -> p t b w", t=4, w=2),
             )
 
-        def perm_resp(h, g):
-            nc.vector.tensor_copy(
-                out=resp_perm[h][:, g, :].bitcast(I32).rearrange("p (t b w) -> p t b w", t=4, w=4),
-                in_=resp_raw[h][:, g, :].bitcast(I32).rearrange("p (b t w) -> p t b w", t=4, w=4),
-            )
+        def perm_resp(grp):
+            for g in range(2):
+                nc.vector.tensor_copy(
+                    out=resp_perm[grp][:, g, :].bitcast(I32).rearrange("p (t b w) -> p t b w", t=4, w=4),
+                    in_=resp_raw[grp][:, g, :].bitcast(I32).rearrange("p (b t w) -> p t b w", t=4, w=4),
+                )
+
+        def vectors():
+            bank = rot.tile([P, 8, P], BF16, name="bank", tag="bank")
+            for grp in range(GROUPS):
+                cols = slice(128 * grp, 128 * (grp + 1))
+                nc.tensor.transpose(bank[:, grp, :], vec_b[:, cols], ident_b[:])
+            nc.vector.tensor_copy(out=vec_t[:], in_=bank[:, 0:GROUPS, 0:8])
 
         inc_wid, inc_grp = {}, {}
 
         def widen(grp):
             wid = work.tile([P, 4, 512], BF16, name="inc_wid", tag="inc_wid", align_bytes=64)
             inc_wid[grp] = wid
-            lo = 512 * (grp % 2)
             for j in range(4):
                 nc.vector.tensor_scalar(
                     out=wid[:, j, :].rearrange("p (t q i) -> p q t i", t=4, i=8),
-                    in0=inc_b[grp // 2][:, j, lo : lo + 512].bitcast(FP8).rearrange("p (q t i) -> p q t i", t=4, i=8),
+                    in0=inc_b[grp][:, j, :].bitcast(FP8).rearrange("p (q t i) -> p q t i", t=4, i=8),
                     scalar1=inc_sc[:, j : j + 1],
                     scalar2=None,
                     op0=MULT,
@@ -216,14 +228,13 @@ def tile_active_surface_link_s11_kernel(
                     [P, HALF_R, 4], BF16, name="outg", tag="outg", bufs=6, align_bytes=64
                 )
             bank = rot.tile([P, 512], F32, name="bank", tag="bank")
-            half, local = grp // 2, grp % 2
             for t in range(4):
-                lo = 512 * t + 256 * local
+                lo = 256 * t
                 so = 512 * t + 128 * grp
                 for g in range(2):
                     nc.tensor.matmul_mx(
                         out=bank[:, 128 * t : 128 * (t + 1)],
-                        lhsT=resp_perm[half][:, g, lo : lo + 256].bitcast(FP4X4),
+                        lhsT=resp_perm[grp][:, g, lo : lo + 256].bitcast(FP4X4),
                         lhsT_scale=rs_perm[:, g, so : so + 128],
                         rhs=coef_codes[n][:, g, :].bitcast(FP8X4),
                         rhs_scale=coef_scales[n][:, g, :],
@@ -256,17 +267,15 @@ def tile_active_surface_link_s11_kernel(
                     start=True,
                     stop=True,
                 )
-                col = 4 * grp + t
-                nc.scalar.activation(th[:, t, :], bank[:], TANH, bias=vec_t[:, col : col + 1])
+                nc.scalar.activation(th[:, t, :], bank[:], TANH, bias=vec_t[:, grp, t : t + 1])
 
         def apply_gain(grp):
             rf = work.tile([P, T, 4], BF16, name="refl", tag="refl", bufs=2, align_bytes=64)
             refl_grp[grp] = rf
-            col = 16 + 4 * grp
             nc.vector.tensor_tensor(
                 out=rf[:],
                 in0=refl_tanh[grp][:].rearrange("p t n -> p n t"),
-                in1=vec_t[:, col : col + 4].unsqueeze(1).to_broadcast([P, T, 4]),
+                in1=vec_t[:, grp, 4:8].unsqueeze(1).to_broadcast([P, T, 4]),
                 op=MULT,
             )
 
@@ -277,123 +286,126 @@ def tile_active_surface_link_s11_kernel(
                 in_=refl_grp[grp][:].rearrange("p n t -> p (n t)"),
             )
 
-        def final_pass(h, m, grp, bank):
+        def final_pass(h, m, grp, bank, recv=slice(0, HALF_R)):
             cols = slice(128 * m, 128 * (m + 1))
             nc.tensor.matmul_mx(
-                out=bank[:],
+                out=bank[:, recv],
                 lhsT=refl_codes[grp][:, cols].bitcast(FP8X4),
                 lhsT_scale=refl_scales[grp][:, cols],
-                rhs=outg_codes[h][grp][:].bitcast(FP8X4),
-                rhs_scale=outg_scales[h][grp][:],
+                rhs=outg_codes[h][grp][:, recv].bitcast(FP8X4),
+                rhs_scale=outg_scales[h][grp][:, recv],
                 start=(grp == 0),
                 stop=(grp == GROUPS - 1),
             )
 
-        def store(h, m, bank, engine):
-            res = work.tile([P, HALF_R], F32, name="res", tag="res", bufs=4, align_bytes=64)
-            copy(engine, res[:], bank[:])
-            nc.sync.dma_start(out=out[128 * m : 128 * (m + 1), HALF_R * h : HALF_R * (h + 1)], in_=res[:])
+        def store(h, m, bank, engine, recv=slice(0, HALF_R)):
+            res = work.tile([P, HALF_R], F32, name="res", tag="res", bufs=8, align_bytes=64)
+            copy(engine, res[:, recv], bank[:, recv])
+            nc.sync.dma_start(
+                out=out[128 * m : 128 * (m + 1), HALF_R * h + recv.start : HALF_R * h + recv.stop], in_=res[:, recv]
+            )
 
         t_coef(0, acc)
-        t_coef(1, acc)
-        c_coef(0, "v")
-        c_coef(1, "s")
-        q_coef(0)
-        q_coef(1)
+        c_coef(0, "s")
         perm_scales(0)
         perm_scales(1)
-        perm_resp(0, 0)
-        perm_resp(0, 1)
-        for n in (0, 1):
-            for grp in (0, 1):
-                outgoing(n, grp, "s")
-        perm_resp(1, 0)
-        perm_resp(1, 1)
-        nc.vector.tensor_copy(out=vec_f[:], in_=vec_b[:])
-        for n in (0, 1):
-            for grp in (2, 3):
-                outgoing(n, grp, "s")
+        q_coef(0)
+        perm_resp(0)
+        outgoing(0, 0, "s")
+        perm_resp(1)
+        outgoing(0, 1, "s")
+        widen(0)
+        t_coef(1, acc)
+        c_coef(1, "s")
+        perm_resp(2)
+        q_coef(1)
+        outgoing(0, 2, "s")
+        perm_resp(3)
+        interleave(0)
+        outgoing(1, 0, "s")
+        outgoing(1, 1, "s")
+        outgoing(0, 3, "s")
+        widen(1)
+        q_inc(0)
         t_coef(2, acc)
         t_coef(3, acc)
-        t_sig(0, acc)
-        t_sig(1, acc)
-        vbank = rot.tile([P, 512], F32, name="bank", tag="bank")
-        nc.tensor.transpose(vbank[:, 0:128], vec_f[:], ident[:])
-        widen(0)
         c_coef(2, "s")
         c_coef(3, "s")
-        interleave(0)
+        outgoing(1, 2, "s")
         q_coef(2)
+        outgoing(1, 3, "s")
         q_coef(3)
-        c_sig(0, "v")
-        c_sig(1, "v")
-        nc.vector.tensor_copy(out=vec_t[:], in_=vbank[:, 0:32])
-        q_inc(0)
-        q_sig()
-        widen(1)
         interleave(1)
+        t_sig(0, acc)
+        t_sig(1, acc)
+        vectors()
+        c_sig(0, "s")
+        c_sig(1, "s")
+        q_inc(1)
+        q_sig()
         for grp in range(4):
             outgoing(2, grp, "s")
-        field(0)
         widen(2)
-        q_inc(1)
         interleave(2)
-        outgoing(3, 0, "s")
-        outgoing(3, 1, "s")
-        field(1)
-        apply_gain(0)
-        q_inc(2)
-        outgoing(3, 2, "s")
-        outgoing(3, 3, "s")
-        q_refl(0)
-        q_outg(0, 0)
-        apply_gain(1)
-        q_outg(0, 1)
-        for n in range(4, 8):
-            t_coef(n, acc)
-        c_coef(4, "s")
-        c_coef(5, "v")
-        c_coef(6, "s")
-        c_coef(7, "v")
-        q_coef(4)
-        q_coef(5)
-        q_coef(6)
-        q_coef(7)
-        q_refl(1)
-        q_outg(0, 2)
-        q_outg(0, 3)
+        field(0)
         widen(3)
-        for n in range(4, 8):
-            outgoing(n, 0, "s")
+        q_inc(2)
+        for grp in range(2):
+            outgoing(3, grp, "s")
         interleave(3)
-        field(2)
-        q_outg(1, 0)
+        apply_gain(0)
         q_inc(3)
         for n in range(4, 8):
+            t_coef(n, acc)
+        for n in range(4, 8):
+            c_coef(n, "s")
+        q_refl(0)
+        for grp in range(2, 4):
+            outgoing(3, grp, "s")
+        for n in range(4, 8):
+            q_coef(n)
+        field(1)
+        q_outg(0, 0)
+        q_outg(0, 1)
+        for n in range(4, 8):
+            outgoing(n, 0, "s")
+        apply_gain(1)
+        q_outg(0, 2)
+        q_outg(0, 3)
+        q_refl(1)
+        field(2)
+        for n in range(4, 8):
             outgoing(n, 1, "s")
+        q_outg(1, 0)
+        apply_gain(2)
+        field(3)
+        q_refl(2)
         fin = [acc.tile([P, 512], F32, name="bank", tag="bank") for m in range(4)]
         for grp in (0, 1):
             for m in range(4):
                 final_pass(0, m, grp, fin[m])
-        apply_gain(2)
         q_outg(1, 1)
-        field(3)
         for n in range(4, 8):
             outgoing(n, 2, "s")
-        q_refl(2)
         apply_gain(3)
         q_outg(1, 2)
         q_refl(3)
         for n in range(4, 8):
             outgoing(n, 3, "v" if n % 2 else "s")
-        for grp in (2, 3):
-            for m in range(4):
-                final_pass(0, m, grp, fin[m])
         q_outg(1, 3)
         for m in range(4):
-            store(0, m, fin[m], "v" if m % 2 else "s")
+            for grp in (2, 3):
+                final_pass(0, m, grp, fin[m])
         for m in range(4):
+            store(0, m, fin[m], "v" if m % 2 else "s")
+        for m in range(3):
             bank = rot.tile([P, 512], F32, name="bank", tag="bank")
             for grp in range(GROUPS):
                 final_pass(1, m, grp, bank)
             store(1, m, bank, "v" if m % 2 else "s")
+        for part in range(2):
+            bank = rot.tile([P, 512], F32, name="bank", tag="bank")
+            cols = slice(256 * part, 256 * (part + 1))
+            for grp in range(GROUPS):
+                final_pass(1, 3, grp, bank, cols)
+            store(1, 3, bank, "s" if part else "v", cols)

@@ -273,9 +273,9 @@ def tile_active_surface_link_s11_kernel(
             rf = work.tile([P, T, 4], BF16, name="refl", tag="refl", bufs=2, align_bytes=64)
             refl_grp[grp] = rf
             nc.vector.tensor_tensor(
-                out=rf[:],
-                in0=refl_tanh[grp][:].rearrange("p t n -> p n t"),
-                in1=vec_t[:, grp, 4:8].unsqueeze(1).to_broadcast([P, T, 4]),
+                out=rf[:].rearrange("p (c i) t -> p c t i", i=4),
+                in0=refl_tanh[grp][:].rearrange("p t (c i) -> p c t i", i=4),
+                in1=vec_t[:, grp, 4:8].unsqueeze(1).unsqueeze(3).to_broadcast([P, T // 4, 4, 4]),
                 op=MULT,
             )
 

from contextlib import ExitStack

import concourse.mybir as mybir
from concourse.masks import make_identity

T, A, E, PATHS, R = 512, 512, 2048, 1024, 1024
FLOPS = 2 * (T * A * E + R * PATHS * E + T * E * R)

F32 = mybir.dt.float32
BF16 = mybir.dt.bfloat16
I32 = mybir.dt.int32
U32 = mybir.dt.uint32
U8 = mybir.dt.uint8
FP8 = mybir.dt.float8_e4m3fn
FP8X4 = mybir.dt.float8_e4m3fn_x4
FP4X4 = mybir.dt.float4_e2m1fn_x4
MULT = mybir.AluOpType.mult
TANH = mybir.ActivationFunctionType.Tanh

P = 128
GROUPS = E // 512
N_COEF = R // 128
HALF_R = 512


def tile_active_surface_link_s11_kernel(
    tc, sig, inc_bytes, inc_scale, bias, gain, coef, resp_words, resp_scales, out
):
    nc = tc.nc
    with ExitStack() as ctx:
        keep = ctx.enter_context(tc.tile_pool(name="keep", bufs=1))
        work = ctx.enter_context(tc.tile_pool(name="work", bufs=2))
        rot = ctx.enter_context(tc.psum_pool(name="rot", bufs=4))
        acc = ctx.enter_context(tc.psum_pool(name="acc", bufs=4))
        ctx.enter_context(tc.manual_schedule())

        def kept(name, shape, dtype):
            return keep.tile(shape, dtype, name=name, tag=name, align_bytes=64)

        coef_raw = [kept("coef_raw%d" % n, [P, PATHS], BF16) for n in range(N_COEF)]
        coef_codes = [kept("coef_codes%d" % n, [P, 2, 128], U32) for n in range(N_COEF)]
        coef_scales = [kept("coef_scales%d" % n, [P, 2, 128], U8) for n in range(N_COEF)]
        resp_raw = [kept("resp_raw%d" % g, [P, 2, 1024], U8) for g in range(GROUPS)]
        resp_perm = [kept("resp_perm%d" % g, [P, 2, 1024], U8) for g in range(GROUPS)]
        rs_raw = kept("rs_raw", [P, 2, E], U8)
        rs_perm = kept("rs_perm", [P, 2, E], U8)
        inc_b = [kept("inc_b%d" % g, [P, 4, 512], U8) for g in range(GROUPS)]
        inc_sc = kept("inc_sc", [P, 4], F32)
        inc_codes = [kept("inc_codes%d" % g, [P, 512], U32) for g in range(GROUPS)]
        inc_scales = [kept("inc_scales%d" % g, [P, 512], U8) for g in range(GROUPS)]
        sig_raw = kept("sig_raw", [P, 4, A], BF16)
        sig_grp = kept("sig_grp", [P, T, 4], BF16)
        sig_codes = kept("sig_codes", [P, T], U32)
        sig_scales = kept("sig_scales", [P, T], U8)
        refl_codes = [kept("refl_codes%d" % g, [P, T], U32) for g in range(GROUPS)]
        refl_scales = [kept("refl_scales%d" % g, [P, T], U8) for g in range(GROUPS)]
        outg_codes = [[kept("outg_codes%d_%d" % (h, g), [P, HALF_R], U32) for g in range(GROUPS)] for h in range(2)]
        outg_scales = [[kept("outg_scales%d_%d" % (h, g), [P, HALF_R], U8) for g in range(GROUPS)] for h in range(2)]
        ident = kept("ident", [P, P], F32)
        ident_b = kept("ident_b", [P, P], BF16)
        vec_b = kept("vec_b", [P, 512], BF16)
        vec_t = kept("vec_t", [P, GROUPS, 8], F32)
        dummy = kept("dummy", [P, 1], F32)

        nc.vector.memset(rs_raw[:].rearrange("p g e -> p (g e)").bitcast(I32), 0)
        nc.vector.memset(dummy[:], 0.0)
        make_identity(nc, ident[:])
        nc.gpsimd.memset(vec_b[:], 0.0)
        make_identity(nc, ident_b[:])
        nc.scalar.activation(dummy[:], dummy[:], TANH)

        def load_coef(n):
            nc.sync.dma_start(out=coef_raw[n][:], in_=coef[128 * n : 128 * (n + 1), :])

        def load_resp(grp):
            nc.sync.dma_start(
                out=resp_raw[grp][:].bitcast(I32),
                in_=resp_words[:, :, 1024 * grp : 1024 * (grp + 1)].rearrange("g p b -> p g b").bitcast(I32),
            )

        def load_inc(grp):
            cols = slice(512 * grp, 512 * (grp + 1))
            nc.sync.dma_start(out=inc_b[grp][:], in_=inc_bytes[:, cols].rearrange("(p j) e -> p j e", j=4))

        for v, vec in enumerate((bias, gain)):
            nc.scalar.dma_start(
                out=vec_b[4 * v : 4 * v + 4, :].rearrange("t (b i) -> t b i", i=8),
                in_=vec.rearrange("(b t i) -> t b i", t=4, i=8),
            )
        load_coef(0)
        for q in range(4):
            nc.sync.dma_start(
                out=rs_raw[32 * q : 32 * q + 4, :, :].bitcast(I32),
                in_=resp_scales[:, 4 * q : 4 * q + 4, :].rearrange("g q e -> q g e").bitcast(I32),
            )
        load_resp(0)
        load_resp(1)
        nc.sync.dma_start(out=inc_sc[:], in_=inc_scale.rearrange("(p j) o -> p (j o)", j=4))
        load_inc(0)
        load_coef(1)
        load_resp(2)
        load_resp(3)
        load_inc(1)
        load_coef(2)
        load_coef(3)
        nc.sync.dma_start(out=sig_raw[:], in_=sig.rearrange("(n p) a -> p n a", p=P))
        load_inc(2)
        load_inc(3)
        load_coef(4)
        load_coef(5)
        load_coef(6)
        load_coef(7)

        coef_bank, coef_grp = {}, {}

        def t_coef(n, pool):
            bank = pool.tile([P, 512], F32, name="bank", tag="bank")
            words = coef_raw[n][:].bitcast(F32)
            for g in range(2):
                for u in range(2):
                    j = 2 * g + u
                    nc.tensor.transpose(
                        bank[:, 128 * j : 128 * (j + 1)], words[:, 256 * g + u : 256 * (g + 1) : 2], ident[:]
                    )
            coef_bank[n] = bank

        def copy(engine, dst, src):
            if engine == "v":
                nc.vector.tensor_copy(out=dst, in_=src)
            else:
                nc.scalar.copy(out=dst, in_=src)

        def c_coef(n, engine):
            grp = work.tile([P, 2, 128, 4], BF16, name="coef_grp", tag="coef_grp", bufs=4, align_bytes=64)
            coef_grp[n] = grp
            copy(
                engine,
                grp[:].rearrange("p g r t -> p (g r t)").bitcast(F32).rearrange("p (g r u) -> p g r u", g=2, u=2),
                coef_bank[n][:].rearrange("p (g u r) -> p g r u", g=2, u=2),
            )

        def q_coef(n):
            nc.vector.quantize_mx(
                out=coef_codes[n][:].rearrange("p g r -> p (g r)").bitcast(FP8X4),
                scales=coef_scales[n][:].rearrange("p g r -> p (g r)"),
                in_=coef_grp[n][:].rearrange("p g r t -> p (g r t)"),
            )

        sig_bank = {}

        def t_sig(pair, pool):
            bank = pool.tile([P, 512], F32, name="bank", tag="bank")
            for i in range(2):
                words = sig_raw[:, 2 * pair + i, :].bitcast(F32)
                for u in range(2):
                    j = 2 * i + u
                    nc.tensor.transpose(bank[:, 128 * j : 128 * (j + 1)], words[:, u:256:2], ident[:])
            sig_bank[pair] = bank

        def c_sig(pair, engine):
            dst = sig_grp[:, 256 * pair : 256 * (pair + 1), :].rearrange("p r t -> p (r t)").bitcast(F32)
            copy(
                engine,
                dst.rearrange("p (i r u) -> p i r u", i=2, u=2),
                sig_bank[pair][:].rearrange("p (i u r) -> p i r u", i=2, u=2),
            )

        def q_sig():
            nc.vector.quantize_mx(
                out=sig_codes[:].bitcast(FP8X4), scales=sig_scales[:], in_=sig_grp[:].rearrange("p r t -> p (r t)")
            )

        def perm_scales(g):
            nc.vector.tensor_copy(
                out=rs_perm[:, g, :].bitcast(I32).rearrange("p (t b w) -> p t b w", t=4, w=2),
                in_=rs_raw[:, g, :].bitcast(I32).rearrange("p (b t w) -> p t b w", t=4, w=2),
            )

        def perm_resp(grp):
            for g in range(2):
                nc.vector.tensor_copy(
                    out=resp_perm[grp][:, g, :].bitcast(I32).rearrange("p (t b w) -> p t b w", t=4, w=4),
                    in_=resp_raw[grp][:, g, :].bitcast(I32).rearrange("p (b t w) -> p t b w", t=4, w=4),
                )

        def vectors():
            bank = rot.tile([P, 8, P], BF16, name="bank", tag="bank")
            for grp in range(GROUPS):
                cols = slice(128 * grp, 128 * (grp + 1))
                nc.tensor.transpose(bank[:, grp, :], vec_b[:, cols], ident_b[:])
            nc.vector.tensor_copy(out=vec_t[:], in_=bank[:, 0:GROUPS, 0:8])

        inc_wid, inc_grp = {}, {}

        def widen(grp):
            wid = work.tile([P, 4, 512], BF16, name="inc_wid", tag="inc_wid", align_bytes=64)
            inc_wid[grp] = wid
            for j in range(4):
                nc.vector.tensor_scalar(
                    out=wid[:, j, :].rearrange("p (t q i) -> p q t i", t=4, i=8),
                    in0=inc_b[grp][:, j, :].bitcast(FP8).rearrange("p (q t i) -> p q t i", t=4, i=8),
                    scalar1=inc_sc[:, j : j + 1],
                    scalar2=None,
                    op0=MULT,
                )

        def interleave(grp):
            g4 = work.tile([P, 512, 4], BF16, name="inc_grp", tag="inc_grp", align_bytes=64)
            inc_grp[grp] = g4
            nc.vector.tensor_copy(
                out=g4[:].rearrange("p (c i) j -> p c j i", i=4),
                in_=inc_wid[grp][:].rearrange("p j (c i) -> p c j i", i=4),
            )

        def q_inc(grp):
            nc.vector.quantize_mx(
                out=inc_codes[grp][:].bitcast(FP8X4),
                scales=inc_scales[grp][:],
                in_=inc_grp[grp][:].rearrange("p c j -> p (c j)"),
            )

        outg = {}

        def outgoing(n, grp, engine):
            h = n // 4
            if (h, grp) not in outg:
                outg[(h, grp)] = work.tile(
                    [P, HALF_R, 4], BF16, name="outg", tag="outg", bufs=6, align_bytes=64
                )
            bank = rot.tile([P, 512], F32, name="bank", tag="bank")
            for t in range(4):
                lo = 256 * t
                so = 512 * t + 128 * grp
                for g in range(2):
                    nc.tensor.matmul_mx(
                        out=bank[:, 128 * t : 128 * (t + 1)],
                        lhsT=resp_perm[grp][:, g, lo : lo + 256].bitcast(FP4X4),
                        lhsT_scale=rs_perm[:, g, so : so + 128],
                        rhs=coef_codes[n][:, g, :].bitcast(FP8X4),
                        rhs_scale=coef_scales[n][:, g, :],
                        start=(g == 0),
                        stop=(g == 1),
                    )
            r0 = 128 * (n % 4)
            copy(engine, outg[(h, grp)][:, r0 : r0 + 128, :], bank[:].rearrange("p (t r) -> p r t", t=4))

        def q_outg(h, grp):
            nc.vector.quantize_mx(
                out=outg_codes[h][grp][:].bitcast(FP8X4),
                scales=outg_scales[h][grp][:],
                in_=outg[(h, grp)][:].rearrange("p r t -> p (r t)"),
            )

        refl_tanh, refl_grp = {}, {}

        def field(grp):
            th = work.tile([P, 4, T], F32, name="th", tag="th", bufs=3, align_bytes=64)
            refl_tanh[grp] = th
            for t in range(4):
                bank = rot.tile([P, 512], F32, name="bank", tag="bank")
                nc.tensor.matmul_mx(
                    out=bank[:],
                    lhsT=inc_codes[grp][:, 128 * t : 128 * (t + 1)].bitcast(FP8X4),
                    lhsT_scale=inc_scales[grp][:, 128 * t : 128 * (t + 1)],
                    rhs=sig_codes[:].bitcast(FP8X4),
                    rhs_scale=sig_scales[:],
                    start=True,
                    stop=True,
                )
                nc.scalar.activation(th[:, t, :], bank[:], TANH, bias=vec_t[:, grp, t : t + 1])

        def apply_gain(grp):
            rf = work.tile([P, T, 4], BF16, name="refl", tag="refl", bufs=2, align_bytes=64)
            refl_grp[grp] = rf
            nc.vector.tensor_tensor(
                out=rf[:].rearrange("p (c i) t -> p c t i", i=4),
                in0=refl_tanh[grp][:].rearrange("p t (c i) -> p c t i", i=4),
                in1=vec_t[:, grp, 4:8].unsqueeze(1).unsqueeze(3).to_broadcast([P, T // 4, 4, 4]),
                op=MULT,
            )

        def q_refl(grp):
            nc.vector.quantize_mx(
                out=refl_codes[grp][:].bitcast(FP8X4),
                scales=refl_scales[grp][:],
                in_=refl_grp[grp][:].rearrange("p n t -> p (n t)"),
            )

        def final_pass(h, m, grp, bank, recv=slice(0, HALF_R)):
            cols = slice(128 * m, 128 * (m + 1))
            nc.tensor.matmul_mx(
                out=bank[:, recv],
                lhsT=refl_codes[grp][:, cols].bitcast(FP8X4),
                lhsT_scale=refl_scales[grp][:, cols],
                rhs=outg_codes[h][grp][:, recv].bitcast(FP8X4),
                rhs_scale=outg_scales[h][grp][:, recv],
                start=(grp == 0),
                stop=(grp == GROUPS - 1),
            )

        def store(h, m, bank, engine, recv=slice(0, HALF_R)):
            res = work.tile([P, HALF_R], F32, name="res", tag="res", bufs=8, align_bytes=64)
            copy(engine, res[:, recv], bank[:, recv])
            nc.sync.dma_start(
                out=out[128 * m : 128 * (m + 1), HALF_R * h + recv.start : HALF_R * h + recv.stop], in_=res[:, recv]
            )

        t_coef(0, acc)
        c_coef(0, "s")
        perm_scales(0)
        perm_scales(1)
        q_coef(0)
        perm_resp(0)
        outgoing(0, 0, "s")
        perm_resp(1)
        outgoing(0, 1, "s")
        widen(0)
        t_coef(1, acc)
        c_coef(1, "s")
        perm_resp(2)
        q_coef(1)
        outgoing(0, 2, "s")
        perm_resp(3)
        interleave(0)
        outgoing(1, 0, "s")
        outgoing(1, 1, "s")
        outgoing(0, 3, "s")
        widen(1)
        q_inc(0)
        t_coef(2, acc)
        t_coef(3, acc)
        c_coef(2, "s")
        c_coef(3, "s")
        outgoing(1, 2, "s")
        q_coef(2)
        outgoing(1, 3, "s")
        q_coef(3)
        interleave(1)
        t_sig(0, acc)
        t_sig(1, acc)
        vectors()
        c_sig(0, "s")
        c_sig(1, "s")
        q_inc(1)
        q_sig()
        for grp in range(4):
            outgoing(2, grp, "s")
        widen(2)
        interleave(2)
        field(0)
        widen(3)
        q_inc(2)
        for grp in range(2):
            outgoing(3, grp, "s")
        interleave(3)
        apply_gain(0)
        q_inc(3)
        for n in range(4, 8):
            t_coef(n, acc)
        for n in range(4, 8):
            c_coef(n, "s")
        q_refl(0)
        for grp in range(2, 4):
            outgoing(3, grp, "s")
        for n in range(4, 8):
            q_coef(n)
        field(1)
        q_outg(0, 0)
        q_outg(0, 1)
        for n in range(4, 8):
            outgoing(n, 0, "s")
        apply_gain(1)
        q_outg(0, 2)
        q_outg(0, 3)
        q_refl(1)
        field(2)
        for n in range(4, 8):
            outgoing(n, 1, "s")
        q_outg(1, 0)
        apply_gain(2)
        field(3)
        q_refl(2)
        fin = [acc.tile([P, 512], F32, name="bank", tag="bank") for m in range(4)]
        for grp in (0, 1):
            for m in range(4):
                final_pass(0, m, grp, fin[m])
        q_outg(1, 1)
        for n in range(4, 8):
            outgoing(n, 2, "s")
        apply_gain(3)
        q_outg(1, 2)
        q_refl(3)
        for n in range(4, 8):
            outgoing(n, 3, "v" if n % 2 else "s")
        q_outg(1, 3)
        for m in range(4):
            for grp in (2, 3):
                final_pass(0, m, grp, fin[m])
        for m in range(4):
            store(0, m, fin[m], "v" if m % 2 else "s")
        for m in range(3):
            bank = rot.tile([P, 512], F32, name="bank", tag="bank")
            for grp in range(GROUPS):
                final_pass(1, m, grp, bank)
            store(1, m, bank, "v" if m % 2 else "s")
        for part in range(2):
            bank = rot.tile([P, 512], F32, name="bank", tag="bank")
            cols = slice(256 * part, 256 * (part + 1))
            for grp in range(GROUPS):
                final_pass(1, 3, grp, bank, cols)
            store(1, 3, bank, "s" if part else "v", cols)
